import numpy as np
import ml_dtypes


def mxq(x, axis, fmt="e4m3"):
    dtype, down = {"e4m3": (ml_dtypes.float8_e4m3fn, 7), "e5m2": (ml_dtypes.float8_e5m2, 14)}[fmt]
    v = np.moveaxis(np.asarray(x, np.float32).astype(ml_dtypes.bfloat16).astype(np.float64), axis, -1)
    blocks = v.reshape(v.shape[:-1] + (-1, 32))
    amax = np.abs(blocks).max(-1, keepdims=True)
    byte = np.maximum(np.where(amax > 0, np.frexp(amax)[1] - 1 + 127, 0) - down, 1)
    scale = np.exp2(byte - 127.0)
    codes = (blocks / scale).astype(np.float32).astype(dtype).astype(np.float64)
    return np.moveaxis((codes * scale).reshape(v.shape), -1, axis)


WIDE = False


def mx_kscale(k):
    if not WIDE:
        return np.ones(k)
    levels = np.array([30, -30])
    if k % 512:
        return np.exp2(np.random.permutation(np.resize(levels, k // 32))).repeat(32)
    a = np.empty((k // 512, 16))
    for p in range(k // 512):
        a[p, :8] = np.random.permutation(np.resize(levels, 8))
        for g in range(8):
            far = levels[np.abs(levels - a[p, g]) >= 10]
            a[p, g + 8] = far[np.random.randint(len(far))]
    return np.exp2(a.ravel()).repeat(32)


def f64(x):
    return np.asarray(x).astype(np.float64)


def striped(idx):
    return np.tile(np.asarray(idx).reshape(-1, 16).T, (8, 1)).astype(np.uint16)


def unstriped(offs):
    return offs[:16].T.reshape(-1).astype(np.int64)


E2M1 = np.array([0.0, 0.5, 1.0, 1.5, 2.0, 3.0, 4.0, 6.0, -0.0, -0.5, -1.0, -1.5, -2.0, -3.0, -4.0, -6.0])


def pack_weight(w, fmt):
    k, n = w.shape
    w = f64(np.asarray(w, np.float32).astype(ml_dtypes.bfloat16)).reshape(k // 32, 32, n)
    amax = np.abs(w).max(1)
    if fmt in ("e4m3", "e5m2"):
        byte = np.frexp(amax)[1] - 1 + 127 - (7 if fmt == "e4m3" else 14)
    else:
        mant, ex = np.frexp(amax / 6.0)
        byte = np.where(mant > 0.5, ex, ex - 1) + 127
    byte = np.clip(np.where(amax > 0, byte, 1), 1, 254)
    scaled = (w * np.exp2(127.0 - byte)[:, None, :]).reshape(k, n).astype(np.float32)
    by_word = np.ascontiguousarray(scaled.reshape(k // 512, 128, 4, n).transpose(0, 1, 3, 2))
    if fmt in ("e4m3", "e5m2"):
        words = by_word.astype(ml_dtypes.float8_e4m3fn if fmt == "e4m3" else ml_dtypes.float8_e5m2).view(np.uint8)
    else:
        c = by_word.astype(ml_dtypes.float4_e2m1fn).view(np.uint8) & 0xF
        words = (c[..., 0::2] | (c[..., 1::2] << 4)).reshape(k // 512, 128, 2 * n)
    return np.ascontiguousarray(words), np.ascontiguousarray(byte.astype(np.uint8).reshape(k // 512, 16, n))


def unpack_weight(words, scales, fmt):
    g, _, n = scales.shape
    words = np.ascontiguousarray(words).reshape(g, 128, n, -1)
    if fmt in ("e4m3", "e5m2"):
        vals = words.view(ml_dtypes.float8_e4m3fn if fmt == "e4m3" else ml_dtypes.float8_e5m2).astype(np.float64)
    else:
        nib = np.empty((g, 128, n, 4), np.uint8)
        nib[..., 0::2] = words & 0xF
        nib[..., 1::2] = words >> 4
        vals = E2M1[nib]
    vals = vals * np.repeat(np.exp2(scales.astype(np.float64) - 127.0), 8, axis=1)[..., None]
    return vals.transpose(0, 1, 3, 2).reshape(g * 512, n)


K, T, Z, J, R, O, N, L, E = 512, 1024, 1024, 256, 512, 128, 256, 512, 1024


def setup_inputs():
    n = np.random.standard_normal
    idx = np.random.permutation(T)[:J]
    idx2 = np.random.permutation(Z)[:J]
    idx3 = np.random.permutation(J)[:O]
    idx4 = np.random.permutation(J)[:O]
    idx5 = np.random.permutation(E)[:O]
    fk = mx_kscale(K)
    fr = mx_kscale(R)
    fl = mx_kscale(L)
    xtp = pack_weight(n((K, T)) / fk[:, None], "e4m3")
    xop = pack_weight(n((K, Z)) / fk[:, None], "e2m1")
    wp = pack_weight(n((K, R)) * 1 / np.sqrt(K) * fk[:, None] * fr, "e5m2")
    wbp = pack_weight(n((R, N)) * 1 / np.sqrt(R) / fr[:, None], "e5m2")
    sxp = pack_weight(n((L, O)) / fl[:, None], "e2m1")
    wsp = pack_weight(n((L, N)) * 1 / np.sqrt(L) * fl[:, None], "e5m2")
    return {
        "xt_words": xtp[0],
        "xt_scales": xtp[1],
        "xo_words": xop[0],
        "xo_scales": xop[1],
        "w_words": wp[0],
        "w_scales": wp[1],
        "wb_words": wbp[0],
        "wb_scales": wbp[1],
        "sx_words": sxp[0],
        "sx_scales": sxp[1],
        "ws_words": wsp[0],
        "ws_scales": wsp[1],
        "offs": striped(idx),
        "offs2": striped(idx2),
        "offs3": striped(idx3),
        "offs4": striped(idx4),
        "offs5": striped(idx5),
    }


def reference(xt_words, xt_scales, xo_words, xo_scales, w_words, w_scales, wb_words, wb_scales, sx_words, sx_scales, ws_words, ws_scales, offs, offs2, offs3, offs4, offs5):
    idx = unstriped(offs)
    idx2 = unstriped(offs2)
    idx3 = unstriped(offs3)
    idx4 = unstriped(offs4)
    idx5 = unstriped(offs5)
    xtu = unpack_weight(xt_words, xt_scales, "e4m3")
    xou = unpack_weight(xo_words, xo_scales, "e2m1")
    wu = unpack_weight(w_words, w_scales, "e5m2")
    wbu = unpack_weight(wb_words, wb_scales, "e5m2")
    sxu = unpack_weight(sx_words, sx_scales, "e2m1")
    wsu = unpack_weight(ws_words, ws_scales, "e5m2")
    xtidxg = xtu[:, idx]
    a = wu.T @ xtidxg
    xoidx2g = xou[:, idx2]
    b = wu.T @ xoidx2g
    hid = np.maximum(a[:, idx3], b[:, idx4])
    hidq = mxq(hid, 0, "e4m3")
    p = wbu.T @ hidq + wsu.T @ sxu
    y = np.zeros((N, E))
    y[:, idx5] = p
    return y

@@ -1,0 +1,158 @@
+from contextlib import ExitStack
+
+import concourse.mybir as mybir
+
+K, T, Z, J, R, O, N, L, E = 512, 1024, 1024, 256, 512, 128, 256, 512, 1024
+FLOPS = 2 * (2 * K * R * J + R * N * O + L * N * O)
+
+F32 = mybir.dt.float32
+BF16 = mybir.dt.bfloat16
+I32 = mybir.dt.int32
+U32 = mybir.dt.uint32
+U16 = mybir.dt.uint16
+U8 = mybir.dt.uint8
+E4M3 = mybir.dt.float8_e4m3fn_x4
+E5M2 = mybir.dt.float8_e5m2_x4
+E2M1 = mybir.dt.float4_e2m1fn_x4
+COPY = mybir.ActivationFunctionType.Copy
+MAX = mybir.AluOpType.max
+
+P = 128
+PACK = 4
+
+
+def load_scale_rows(queue, plane, scales):
+    for q in range(4):
+        queue.dma_start(out=plane[32 * q : 32 * q + 4, :].bitcast(I32), in_=scales[0, 4 * q : 4 * q + 4, :].bitcast(I32))
+
+
+def load_scale_rows_all(queues, plane, scales):
+    for q in range(4):
+        rows = scales[0, 4 * q : 4 * q + 4, :].bitcast(I32)
+        queues[q].dma_start(out=plane[32 * q : 32 * q + 32, :].bitcast(I32), in_=rows.unsqueeze(0).broadcast_to([8, 4, rows.shape[1]]))
+
+
+def fp8_words(words):
+    return words[0].rearrange("p c t -> p (c t)").bitcast(I32)
+
+
+def tile_list_oneforboth_looked_skip_scattered_kernel(
+    tc, xt_words, xt_scales, xo_words, xo_scales, w_words, w_scales, wb_words, wb_scales,
+    sx_words, sx_scales, ws_words, ws_scales, offs, offs2, offs3, offs4, offs5, out,
+):
+    nc = tc.nc
+    with ExitStack() as ctx:
+        sb = ctx.enter_context(tc.tile_pool(name="sb", bufs=1))
+        ps = ctx.enter_context(tc.psum_pool(name="ps", bufs=1))
+
+        def tile(name, width, dtype):
+            return sb.tile([P, width], dtype, name=name, align_bytes=64)
+
+        list1 = tile("list1", J // 16, U16)
+        list2 = tile("list2", J // 16, U16)
+        list3 = tile("list3", O // 16, U16)
+        list4 = tile("list4", O // 16, U16)
+        list5 = tile("list5", O // 16, U16)
+        xt_w = tile("xt_w", T, U32)
+        xt_s = tile("xt_s", T, U8)
+        xo_w = tile("xo_w", Z, U16)
+        xo_s = tile("xo_s", Z, U8)
+        w_w = tile("w_w", R, U32)
+        w_s = tile("w_s", R, U8)
+        wb_w = tile("wb_w", N, U32)
+        wb_s = tile("wb_s", N, U8)
+        ws_w = tile("ws_w", N, U32)
+        ws_s = tile("ws_s", N, U8)
+        sx_w = tile("sx_w", 2 * O, U8)
+        sx_s = tile("sx_s", O, U8)
+
+
+        nc.sync.dma_start(list1[:], offs)
+        load_scale_rows_all([nc.sync, nc.sync, nc.scalar, nc.scalar], xt_s, xt_scales)
+        nc.scalar.dma_start(out=xt_w[:].bitcast(I32), in_=fp8_words(xt_words))
+        nc.scalar.dma_start(out=w_w[:].bitcast(I32), in_=fp8_words(w_words))
+        load_scale_rows_all([nc.sync] * 4, w_s, w_scales)
+        nc.scalar.dma_start(out=xo_w[:].bitcast(I32), in_=xo_words[0].bitcast(I32))
+        nc.sync.dma_start(list2[:], offs2)
+        load_scale_rows_all([nc.gpsimd, nc.gpsimd, nc.sync, nc.sync], xo_s, xo_scales)
+        nc.sync.dma_start(list3[:], offs3)
+        nc.sync.dma_start(list4[:], offs4)
+        load_scale_rows(nc.gpsimd, sx_s, sx_scales)
+        load_scale_rows(nc.sync, ws_s, ws_scales)
+        nc.sync.dma_start(out=ws_w[:].bitcast(I32), in_=fp8_words(ws_words))
+        nc.sync.dma_start(out=sx_w[:].bitcast(I32), in_=sx_words[0].bitcast(I32))
+        nc.sync.dma_start(out=wb_w[:].bitcast(I32), in_=fp8_words(wb_words))
+        load_scale_rows(nc.sync, wb_s, wb_scales)
+        nc.sync.dma_start(list5[:], offs5)
+
+        pages = [tile("page%d" % h, E, F32) for h in range(2)]
+        for page in pages:
+            nc.vector.memset(page[:], 0.0)
+
+        xtg_s = tile("xtg_s", J, U8)
+        xtg_w = tile("xtg_w", J, U32)
+        xog_s = tile("xog_s", J, U8)
+        xog_w = tile("xog_w", J, U16)
+        wp_w = tile("wp_w", R, U32)
+        wp_s = tile("wp_s", R, U8)
+        nc.vector.tensor_copy(xtg_s[:], xt_s[:].indirect(list1[:]))
+        nc.vector.tensor_copy(xtg_w[:], xt_w[:].indirect(list1[:]))
+        nc.scalar.copy(out=wp_w[:].rearrange("p (t m) -> p t m", t=PACK), in_=w_w[:].rearrange("p (m t) -> p t m", t=PACK))
+        nc.vector.tensor_copy(out=wp_s[:].rearrange("p (t m) -> p t m", t=PACK), in_=w_s[:].rearrange("p (m t) -> p t m", t=PACK))
+        nc.vector.tensor_copy(xog_w[:], xo_w[:].indirect(list2[:]))
+        nc.vector.tensor_copy(xog_s[:], xo_s[:].indirect(list2[:]))
+
+        def first_product(acc, t, words, scales):
+            cols = slice(P * t, P * (t + 1))
+            nc.tensor.matmul_mx(out=acc, lhsT=wp_w[:, cols].bitcast(E5M2), lhsT_scale=wp_s[:, cols],
+                                rhs=words, rhs_scale=scales, start=True, stop=True)
+
+        ga = tile("ga", PACK * O, F32)
+        gb = tile("gb", PACK * O, F32)
+        for t in range(PACK):
+            bank = ps.tile([P, J], F32, name="a_ps%d" % t, tag="bank%d" % t)
+            first_product(bank[:], t, xtg_w[:].bitcast(E4M3), xtg_s[:])
+            a_sb = tile("a_sb%d" % t, J, F32)
+            nc.scalar.copy(out=a_sb[:], in_=bank[:])
+            nc.scalar.activation(ga[:, O * t : O * (t + 1)], a_sb[:].indirect(list3[:]), COPY)
+        for t in range(PACK):
+            bank = ps.tile([P, J], F32, name="b_ps%d" % t)
+            first_product(bank[:], t, xog_w[:].bitcast(E2M1), xog_s[:])
+            b_sb = tile("b_sb%d" % t, J, F32)
+            if t < 3:
+                nc.vector.tensor_copy(out=b_sb[:], in_=bank[:])
+                nc.vector.tensor_copy(gb[:, O * t : O * (t + 1)], b_sb[:].indirect(list4[:]))
+            else:
+                nc.scalar.copy(out=b_sb[:], in_=bank[:])
+                nc.scalar.activation(gb[:, O * t : O * (t + 1)], b_sb[:].indirect(list4[:]), COPY)
+
+        p_ps = [ps.tile([P, O], F32, name="p_ps%d" % h, tag="bank%d" % h) for h in range(2)]
+        for h in range(2):
+            cols = slice(P * h, P * (h + 1))
+            nc.tensor.matmul_mx(out=p_ps[h][:], lhsT=ws_w[:, cols].bitcast(E5M2), lhsT_scale=ws_s[:, cols],
+                                rhs=sx_w[:].bitcast(E2M1), rhs_scale=sx_s[:], start=True, stop=False)
+
+        hid = tile("hid", PACK * O, BF16)
+        nc.vector.tensor_tensor(
+            hid[:].rearrange("p (c i t) -> p c t i", i=4, t=PACK),
+            ga[:].rearrange("p (t c i) -> p c t i", i=4, t=PACK),
+            gb[:].rearrange("p (t c i) -> p c t i", i=4, t=PACK),
+            MAX,
+        )
+        hid_w = tile("hid_w", O, U32)
+        hid_s = tile("hid_s", O, U8)
+        nc.vector.quantize_mx(out=hid_w[:].bitcast(E4M3), scales=hid_s[:], in_=hid[:])
+
+        for h in range(2):
+            cols = slice(P * h, P * (h + 1))
+            nc.tensor.matmul_mx(out=p_ps[h][:], lhsT=wb_w[:, cols].bitcast(E5M2), lhsT_scale=wb_s[:, cols],
+                                rhs=hid_w[:].bitcast(E4M3), rhs_scale=hid_s[:], start=False, stop=True)
+            p_sb = tile("p_sb%d" % h, O, F32)
+            if h == 0:
+                nc.scalar.copy(out=p_sb[:], in_=p_ps[h][:])
+                nc.scalar.activation(pages[h][:].indirect(list5[:]), p_sb[:], COPY)
+                nc.scalar.dma_start(out=out[cols, :], in_=pages[h][:])
+            else:
+                nc.vector.tensor_copy(out=p_sb[:], in_=p_ps[h][:])
+                nc.vector.tensor_copy(pages[h][:].indirect(list5[:]), p_sb[:])
+                nc.sync.dma_start(out=out[cols, :], in_=pages[h][:])

@@ -21,15 +21,14 @@ P = 128
 PACK = 4
 
 
-def load_scale_rows(queue, plane, scales):
+def load_scale_rows(queues, plane, scales):
     for q in range(4):
-        queue.dma_start(out=plane[32 * q : 32 * q + 4, :].bitcast(I32), in_=scales[0, 4 * q : 4 * q + 4, :].bitcast(I32))
+        queues[q].dma_start(out=plane[32 * q : 32 * q + 4, :].bitcast(I32), in_=scales[0, 4 * q : 4 * q + 4, :].bitcast(I32))
 
 
-def load_scale_rows_all(queues, plane, scales):
-    for q in range(4):
-        rows = scales[0, 4 * q : 4 * q + 4, :].bitcast(I32)
-        queues[q].dma_start(out=plane[32 * q : 32 * q + 32, :].bitcast(I32), in_=rows.unsqueeze(0).broadcast_to([8, 4, rows.shape[1]]))
+def fill_quadrant(queue, plane, scales, q):
+    rows = scales[0, 4 * q : 4 * q + 4, :].bitcast(I32)
+    queue.dma_start(out=plane[32 * q : 32 * q + 32, :].bitcast(I32), in_=rows.unsqueeze(0).broadcast_to([8, 4, rows.shape[1]]))
 
 
 def fp8_words(words):
@@ -67,27 +66,36 @@ def tile_list_oneforboth_looked_skip_scattered_kernel(
         sx_s = tile("sx_s", O, U8)
 
 
+        fill_quadrant(nc.sync, w_s, w_scales, 0)
+        fill_quadrant(nc.scalar, w_s, w_scales, 1)
+        fill_quadrant(nc.sync, w_s, w_scales, 2)
+        fill_quadrant(nc.scalar, w_s, w_scales, 3)
         nc.sync.dma_start(list1[:], offs)
-        load_scale_rows_all([nc.sync, nc.sync, nc.scalar, nc.scalar], xt_s, xt_scales)
-        nc.scalar.dma_start(out=xt_w[:].bitcast(I32), in_=fp8_words(xt_words))
-        nc.scalar.dma_start(out=w_w[:].bitcast(I32), in_=fp8_words(w_words))
-        load_scale_rows_all([nc.sync] * 4, w_s, w_scales)
-        nc.scalar.dma_start(out=xo_w[:].bitcast(I32), in_=xo_words[0].bitcast(I32))
+        fill_quadrant(nc.scalar, xt_s, xt_scales, 0)
+        nc.sync.dma_start(out=xt_w[:].bitcast(I32), in_=fp8_words(xt_words))
+        nc.sync.dma_start(out=w_w[:].bitcast(I32), in_=fp8_words(w_words))
+        fill_quadrant(nc.gpsimd, xo_s, xo_scales, 0)
+        fill_quadrant(nc.gpsimd, xo_s, xo_scales, 1)
+        for q in (1, 2, 3):
+            fill_quadrant(nc.sync, xt_s, xt_scales, q)
+        nc.sync.dma_start(out=xo_w[:].bitcast(I32), in_=xo_words[0].bitcast(I32))
         nc.sync.dma_start(list2[:], offs2)
-        load_scale_rows_all([nc.gpsimd, nc.gpsimd, nc.sync, nc.sync], xo_s, xo_scales)
+        fill_quadrant(nc.sync, xo_s, xo_scales, 2)
+        fill_quadrant(nc.sync, xo_s, xo_scales, 3)
         nc.sync.dma_start(list3[:], offs3)
         nc.sync.dma_start(list4[:], offs4)
-        load_scale_rows(nc.gpsimd, sx_s, sx_scales)
-        load_scale_rows(nc.sync, ws_s, ws_scales)
+        load_scale_rows([nc.gpsimd, nc.gpsimd, nc.sync, nc.sync], sx_s, sx_scales)
+        load_scale_rows([nc.sync] * 4, ws_s, ws_scales)
         nc.sync.dma_start(out=ws_w[:].bitcast(I32), in_=fp8_words(ws_words))
         nc.sync.dma_start(out=sx_w[:].bitcast(I32), in_=sx_words[0].bitcast(I32))
         nc.sync.dma_start(out=wb_w[:].bitcast(I32), in_=fp8_words(wb_words))
-        load_scale_rows(nc.sync, wb_s, wb_scales)
+        load_scale_rows([nc.sync] * 4, wb_s, wb_scales)
         nc.sync.dma_start(list5[:], offs5)
 
         pages = [tile("page%d" % h, E, F32) for h in range(2)]
         for page in pages:
-            nc.vector.memset(page[:], 0.0)
+            nc.vector.memset(page[:, : E // 2 + 1], 0.0)
+            nc.vector.memset(page[:, E // 2 + 1 :], 0.0)
 
         xtg_s = tile("xtg_s", J, U8)
         xtg_w = tile("xtg_w", J, U32)
@@ -95,10 +103,10 @@ def tile_list_oneforboth_looked_skip_scattered_kernel(
         xog_w = tile("xog_w", J, U16)
         wp_w = tile("wp_w", R, U32)
         wp_s = tile("wp_s", R, U8)
-        nc.vector.tensor_copy(xtg_s[:], xt_s[:].indirect(list1[:]))
-        nc.vector.tensor_copy(xtg_w[:], xt_w[:].indirect(list1[:]))
-        nc.scalar.copy(out=wp_w[:].rearrange("p (t m) -> p t m", t=PACK), in_=w_w[:].rearrange("p (m t) -> p t m", t=PACK))
         nc.vector.tensor_copy(out=wp_s[:].rearrange("p (t m) -> p t m", t=PACK), in_=w_s[:].rearrange("p (m t) -> p t m", t=PACK))
+        nc.vector.tensor_copy(xtg_w[:], xt_w[:].indirect(list1[:]))
+        nc.scalar.copy(out=wp_w[:].rearrange("p (t c i) -> p c t i", t=PACK, i=4), in_=w_w[:].rearrange("p (c i t) -> p c t i", t=PACK, i=4))
+        nc.vector.tensor_copy(xtg_s[:], xt_s[:].indirect(list1[:]))
         nc.vector.tensor_copy(xog_w[:], xo_w[:].indirect(list2[:]))
         nc.vector.tensor_copy(xog_s[:], xo_s[:].indirect(list2[:]))
 
@@ -132,16 +140,20 @@ def tile_list_oneforboth_looked_skip_scattered_kernel(
             nc.tensor.matmul_mx(out=p_ps[h][:], lhsT=ws_w[:, cols].bitcast(E5M2), lhsT_scale=ws_s[:, cols],
                                 rhs=sx_w[:].bitcast(E2M1), rhs_scale=sx_s[:], start=True, stop=False)
 
-        hid = tile("hid", PACK * O, BF16)
-        nc.vector.tensor_tensor(
-            hid[:].rearrange("p (c i t) -> p c t i", i=4, t=PACK),
-            ga[:].rearrange("p (t c i) -> p c t i", i=4, t=PACK),
-            gb[:].rearrange("p (t c i) -> p c t i", i=4, t=PACK),
-            MAX,
-        )
+        hid = [tile("hid%d" % u, PACK * O // 2, BF16) for u in range(2)]
+        for u in range(2):
+            places = slice(16 * u, 16 * (u + 1))
+            nc.vector.tensor_tensor(
+                hid[u][:].rearrange("p (c i t) -> p c t i", i=4, t=PACK),
+                ga[:].rearrange("p (t c i) -> p c t i", i=4, t=PACK)[:, places],
+                gb[:].rearrange("p (t c i) -> p c t i", i=4, t=PACK)[:, places],
+                MAX,
+            )
         hid_w = tile("hid_w", O, U32)
         hid_s = tile("hid_s", O, U8)
-        nc.vector.quantize_mx(out=hid_w[:].bitcast(E4M3), scales=hid_s[:], in_=hid[:])
+        for u in range(2):
+            half = slice(O // 2 * u, O // 2 * (u + 1))
+            nc.vector.quantize_mx(out=hid_w[:, half].bitcast(E4M3), scales=hid_s[:, half], in_=hid[u][:])
 
         for h in range(2):
             cols = slice(P * h, P * (h + 1))
@@ -149,10 +161,10 @@ def tile_list_oneforboth_looked_skip_scattered_kernel(
                                 rhs=hid_w[:].bitcast(E4M3), rhs_scale=hid_s[:], start=False, stop=True)
             p_sb = tile("p_sb%d" % h, O, F32)
             if h == 0:
-                nc.scalar.copy(out=p_sb[:], in_=p_ps[h][:])
+                nc.vector.tensor_copy(out=p_sb[:], in_=p_ps[h][:])
                 nc.scalar.activation(pages[h][:].indirect(list5[:]), p_sb[:], COPY)
                 nc.scalar.dma_start(out=out[cols, :], in_=pages[h][:])
             else:
-                nc.vector.tensor_copy(out=p_sb[:], in_=p_ps[h][:])
+                nc.scalar.copy(out=p_sb[:], in_=p_ps[h][:])
                 nc.vector.tensor_copy(pages[h][:].indirect(list5[:]), p_sb[:])
                 nc.sync.dma_start(out=out[cols, :], in_=pages[h][:])

@@ -26,11 +26,6 @@ def load_scale_rows(queues, plane, scales):
         queues[q].dma_start(out=plane[32 * q : 32 * q + 4, :].bitcast(I32), in_=scales[0, 4 * q : 4 * q + 4, :].bitcast(I32))
 
 
-def fill_quadrant(queue, plane, scales, q):
-    rows = scales[0, 4 * q : 4 * q + 4, :].bitcast(I32)
-    queue.dma_start(out=plane[32 * q : 32 * q + 32, :].bitcast(I32), in_=rows.unsqueeze(0).broadcast_to([8, 4, rows.shape[1]]))
-
-
 def fp8_words(words):
     return words[0].rearrange("p c t -> p (c t)").bitcast(I32)
 
@@ -66,30 +61,24 @@ def tile_list_oneforboth_looked_skip_scattered_kernel(
         sx_s = tile("sx_s", O, U8)
 
 
-        fill_quadrant(nc.sync, w_s, w_scales, 0)
-        fill_quadrant(nc.scalar, w_s, w_scales, 1)
-        fill_quadrant(nc.sync, w_s, w_scales, 2)
-        fill_quadrant(nc.scalar, w_s, w_scales, 3)
+        for plane in (w_s, xo_s, xt_s):
+            nc.vector.memset(plane[:].bitcast(I32), 0)
         nc.sync.dma_start(list1[:], offs)
-        fill_quadrant(nc.scalar, xt_s, xt_scales, 0)
+        nc.sync.dma_start(list2[:], offs2)
+        load_scale_rows([nc.sync, nc.scalar, nc.sync, nc.scalar], w_s, w_scales)
         nc.sync.dma_start(out=xt_w[:].bitcast(I32), in_=fp8_words(xt_words))
         nc.sync.dma_start(out=w_w[:].bitcast(I32), in_=fp8_words(w_words))
-        fill_quadrant(nc.gpsimd, xo_s, xo_scales, 0)
-        fill_quadrant(nc.gpsimd, xo_s, xo_scales, 1)
-        for q in (1, 2, 3):
-            fill_quadrant(nc.sync, xt_s, xt_scales, q)
+        load_scale_rows([nc.sync] * 4, xt_s, xt_scales)
         nc.sync.dma_start(out=xo_w[:].bitcast(I32), in_=xo_words[0].bitcast(I32))
-        nc.sync.dma_start(list2[:], offs2)
-        fill_quadrant(nc.sync, xo_s, xo_scales, 2)
-        fill_quadrant(nc.sync, xo_s, xo_scales, 3)
+        load_scale_rows([nc.gpsimd, nc.gpsimd, nc.sync, nc.sync], xo_s, xo_scales)
         nc.sync.dma_start(list3[:], offs3)
         nc.sync.dma_start(list4[:], offs4)
-        load_scale_rows([nc.gpsimd, nc.gpsimd, nc.sync, nc.sync], sx_s, sx_scales)
+        load_scale_rows([nc.gpsimd] * 4, sx_s, sx_scales)
         load_scale_rows([nc.sync] * 4, ws_s, ws_scales)
+        load_scale_rows([nc.sync] * 4, wb_s, wb_scales)
+        nc.sync.dma_start(out=wb_w[:].bitcast(I32), in_=fp8_words(wb_words))
         nc.sync.dma_start(out=ws_w[:].bitcast(I32), in_=fp8_words(ws_words))
         nc.sync.dma_start(out=sx_w[:].bitcast(I32), in_=sx_words[0].bitcast(I32))
-        nc.sync.dma_start(out=wb_w[:].bitcast(I32), in_=fp8_words(wb_words))
-        load_scale_rows([nc.sync] * 4, wb_s, wb_scales)
         nc.sync.dma_start(list5[:], offs5)
 
         pages = [tile("page%d" % h, E, F32) for h in range(2)]

from contextlib import ExitStack

import concourse.mybir as mybir

K, T, Z, J, R, O, N, L, E = 512, 1024, 1024, 256, 512, 128, 256, 512, 1024
FLOPS = 2 * (2 * K * R * J + R * N * O + L * N * O)

F32 = mybir.dt.float32
BF16 = mybir.dt.bfloat16
I32 = mybir.dt.int32
U32 = mybir.dt.uint32
U16 = mybir.dt.uint16
U8 = mybir.dt.uint8
E4M3 = mybir.dt.float8_e4m3fn_x4
E5M2 = mybir.dt.float8_e5m2_x4
E2M1 = mybir.dt.float4_e2m1fn_x4
COPY = mybir.ActivationFunctionType.Copy
MAX = mybir.AluOpType.max

P = 128
PACK = 4


def load_scale_rows(queues, plane, scales):
    for q in range(4):
        queues[q].dma_start(out=plane[32 * q : 32 * q + 4, :].bitcast(I32), in_=scales[0, 4 * q : 4 * q + 4, :].bitcast(I32))


def fp8_words(words):
    return words[0].rearrange("p c t -> p (c t)").bitcast(I32)


def tile_list_oneforboth_looked_skip_scattered_kernel(
    tc, xt_words, xt_scales, xo_words, xo_scales, w_words, w_scales, wb_words, wb_scales,
    sx_words, sx_scales, ws_words, ws_scales, offs, offs2, offs3, offs4, offs5, out,
):
    nc = tc.nc
    with ExitStack() as ctx:
        sb = ctx.enter_context(tc.tile_pool(name="sb", bufs=1))
        ps = ctx.enter_context(tc.psum_pool(name="ps", bufs=1))

        def tile(name, width, dtype):
            return sb.tile([P, width], dtype, name=name, align_bytes=64)

        list1 = tile("list1", J // 16, U16)
        list2 = tile("list2", J // 16, U16)
        list3 = tile("list3", O // 16, U16)
        list4 = tile("list4", O // 16, U16)
        list5 = tile("list5", O // 16, U16)
        xt_w = tile("xt_w", T, U32)
        xt_s = tile("xt_s", T, U8)
        xo_w = tile("xo_w", Z, U16)
        xo_s = tile("xo_s", Z, U8)
        w_w = tile("w_w", R, U32)
        w_s = tile("w_s", R, U8)
        wb_w = tile("wb_w", N, U32)
        wb_s = tile("wb_s", N, U8)
        ws_w = tile("ws_w", N, U32)
        ws_s = tile("ws_s", N, U8)
        sx_w = tile("sx_w", 2 * O, U8)
        sx_s = tile("sx_s", O, U8)


        for plane in (w_s, xo_s, xt_s):
            nc.vector.memset(plane[:].bitcast(I32), 0)
        nc.sync.dma_start(list1[:], offs)
        nc.sync.dma_start(list2[:], offs2)
        load_scale_rows([nc.sync, nc.scalar, nc.sync, nc.scalar], w_s, w_scales)
        nc.sync.dma_start(out=xt_w[:].bitcast(I32), in_=fp8_words(xt_words))
        nc.sync.dma_start(out=w_w[:].bitcast(I32), in_=fp8_words(w_words))
        load_scale_rows([nc.sync] * 4, xt_s, xt_scales)
        nc.sync.dma_start(out=xo_w[:].bitcast(I32), in_=xo_words[0].bitcast(I32))
        load_scale_rows([nc.gpsimd, nc.gpsimd, nc.sync, nc.sync], xo_s, xo_scales)
        nc.sync.dma_start(list3[:], offs3)
        nc.sync.dma_start(list4[:], offs4)
        load_scale_rows([nc.gpsimd] * 4, sx_s, sx_scales)
        load_scale_rows([nc.sync] * 4, ws_s, ws_scales)
        load_scale_rows([nc.sync] * 4, wb_s, wb_scales)
        nc.sync.dma_start(out=wb_w[:].bitcast(I32), in_=fp8_words(wb_words))
        nc.sync.dma_start(out=ws_w[:].bitcast(I32), in_=fp8_words(ws_words))
        nc.sync.dma_start(out=sx_w[:].bitcast(I32), in_=sx_words[0].bitcast(I32))
        nc.sync.dma_start(list5[:], offs5)

        pages = [tile("page%d" % h, E, F32) for h in range(2)]
        for page in pages:
            nc.vector.memset(page[:, : E // 2 + 1], 0.0)
            nc.vector.memset(page[:, E // 2 + 1 :], 0.0)

        xtg_s = tile("xtg_s", J, U8)
        xtg_w = tile("xtg_w", J, U32)
        xog_s = tile("xog_s", J, U8)
        xog_w = tile("xog_w", J, U16)
        wp_w = tile("wp_w", R, U32)
        wp_s = tile("wp_s", R, U8)
        nc.vector.tensor_copy(out=wp_s[:].rearrange("p (t m) -> p t m", t=PACK), in_=w_s[:].rearrange("p (m t) -> p t m", t=PACK))
        nc.vector.tensor_copy(xtg_w[:], xt_w[:].indirect(list1[:]))
        nc.scalar.copy(out=wp_w[:].rearrange("p (t c i) -> p c t i", t=PACK, i=4), in_=w_w[:].rearrange("p (c i t) -> p c t i", t=PACK, i=4))
        nc.vector.tensor_copy(xtg_s[:], xt_s[:].indirect(list1[:]))
        nc.vector.tensor_copy(xog_w[:], xo_w[:].indirect(list2[:]))
        nc.vector.tensor_copy(xog_s[:], xo_s[:].indirect(list2[:]))

        def first_product(acc, t, words, scales):
            cols = slice(P * t, P * (t + 1))
            nc.tensor.matmul_mx(out=acc, lhsT=wp_w[:, cols].bitcast(E5M2), lhsT_scale=wp_s[:, cols],
                                rhs=words, rhs_scale=scales, start=True, stop=True)

        ga = tile("ga", PACK * O, F32)
        gb = tile("gb", PACK * O, F32)
        for t in range(PACK):
            bank = ps.tile([P, J], F32, name="a_ps%d" % t, tag="bank%d" % t)
            first_product(bank[:], t, xtg_w[:].bitcast(E4M3), xtg_s[:])
            a_sb = tile("a_sb%d" % t, J, F32)
            nc.scalar.copy(out=a_sb[:], in_=bank[:])
            nc.scalar.activation(ga[:, O * t : O * (t + 1)], a_sb[:].indirect(list3[:]), COPY)
        for t in range(PACK):
            bank = ps.tile([P, J], F32, name="b_ps%d" % t)
            first_product(bank[:], t, xog_w[:].bitcast(E2M1), xog_s[:])
            b_sb = tile("b_sb%d" % t, J, F32)
            if t < 3:
                nc.vector.tensor_copy(out=b_sb[:], in_=bank[:])
                nc.vector.tensor_copy(gb[:, O * t : O * (t + 1)], b_sb[:].indirect(list4[:]))
            else:
                nc.scalar.copy(out=b_sb[:], in_=bank[:])
                nc.scalar.activation(gb[:, O * t : O * (t + 1)], b_sb[:].indirect(list4[:]), COPY)

        p_ps = [ps.tile([P, O], F32, name="p_ps%d" % h, tag="bank%d" % h) for h in range(2)]
        for h in range(2):
            cols = slice(P * h, P * (h + 1))
            nc.tensor.matmul_mx(out=p_ps[h][:], lhsT=ws_w[:, cols].bitcast(E5M2), lhsT_scale=ws_s[:, cols],
                                rhs=sx_w[:].bitcast(E2M1), rhs_scale=sx_s[:], start=True, stop=False)

        hid = [tile("hid%d" % u, PACK * O // 2, BF16) for u in range(2)]
        for u in range(2):
            places = slice(16 * u, 16 * (u + 1))
            nc.vector.tensor_tensor(
                hid[u][:].rearrange("p (c i t) -> p c t i", i=4, t=PACK),
                ga[:].rearrange("p (t c i) -> p c t i", i=4, t=PACK)[:, places],
                gb[:].rearrange("p (t c i) -> p c t i", i=4, t=PACK)[:, places],
                MAX,
            )
        hid_w = tile("hid_w", O, U32)
        hid_s = tile("hid_s", O, U8)
        for u in range(2):
            half = slice(O // 2 * u, O // 2 * (u + 1))
            nc.vector.quantize_mx(out=hid_w[:, half].bitcast(E4M3), scales=hid_s[:, half], in_=hid[u][:])

        for h in range(2):
            cols = slice(P * h, P * (h + 1))
            nc.tensor.matmul_mx(out=p_ps[h][:], lhsT=wb_w[:, cols].bitcast(E5M2), lhsT_scale=wb_s[:, cols],
                                rhs=hid_w[:].bitcast(E4M3), rhs_scale=hid_s[:], start=False, stop=True)
            p_sb = tile("p_sb%d" % h, O, F32)
            if h == 0:
                nc.vector.tensor_copy(out=p_sb[:], in_=p_ps[h][:])
                nc.scalar.activation(pages[h][:].indirect(list5[:]), p_sb[:], COPY)
                nc.scalar.dma_start(out=out[cols, :], in_=pages[h][:])
            else:
                nc.scalar.copy(out=p_sb[:], in_=p_ps[h][:])
                nc.vector.tensor_copy(pages[h][:].indirect(list5[:]), p_sb[:])
                nc.sync.dma_start(out=out[cols, :], in_=pages[h][:])
